import numpy as np
import ml_dtypes


def mxq(x, axis, fmt="e4m3"):
    dtype, down = {"e4m3": (ml_dtypes.float8_e4m3fn, 7), "e5m2": (ml_dtypes.float8_e5m2, 14)}[fmt]
    v = np.moveaxis(np.asarray(x, np.float32).astype(ml_dtypes.bfloat16).astype(np.float64), axis, -1)
    blocks = v.reshape(v.shape[:-1] + (-1, 32))
    amax = np.abs(blocks).max(-1, keepdims=True)
    byte = np.maximum(np.where(amax > 0, np.frexp(amax)[1] - 1 + 127, 0) - down, 1)
    scale = np.exp2(byte - 127.0)
    codes = (blocks / scale).astype(np.float32).astype(dtype).astype(np.float64)
    return np.moveaxis((codes * scale).reshape(v.shape), -1, axis)


WIDE = False


def mx_kscale(k):
    if not WIDE:
        return np.ones(k)
    levels = np.array([10, -10, 5, -5, 0])
    if k % 512:
        return np.exp2(np.random.permutation(np.resize(levels, k // 32))).repeat(32)
    a = np.empty((k // 512, 16))
    for p in range(k // 512):
        a[p, :8] = np.random.permutation(np.resize(levels, 8))
        for g in range(8):
            far = levels[np.abs(levels - a[p, g]) >= 10]
            a[p, g + 8] = far[np.random.randint(len(far))]
    return np.exp2(a.ravel()).repeat(32)


def f64(x):
    return np.asarray(x).astype(np.float64)


def striped(idx):
    return np.tile(np.asarray(idx).reshape(-1, 16).T, (8, 1)).astype(np.uint16)


def unstriped(offs):
    return offs[:16].T.reshape(-1).astype(np.int64)


E2M1 = np.array([0.0, 0.5, 1.0, 1.5, 2.0, 3.0, 4.0, 6.0, -0.0, -0.5, -1.0, -1.5, -2.0, -3.0, -4.0, -6.0])


def pack_weight(w, fmt):
    k, n = w.shape
    w = f64(np.asarray(w, np.float32).astype(ml_dtypes.bfloat16)).reshape(k // 32, 32, n)
    amax = np.abs(w).max(1)
    if fmt == "e4m3":
        byte = np.frexp(amax)[1] - 1 + 127 - 7
    else:
        mant, ex = np.frexp(amax / 6.0)
        byte = np.where(mant > 0.5, ex, ex - 1) + 127
    byte = np.clip(np.where(amax > 0, byte, 1), 1, 254)
    scaled = (w * np.exp2(127.0 - byte)[:, None, :]).reshape(k, n).astype(np.float32)
    by_word = np.ascontiguousarray(scaled.reshape(k // 512, 128, 4, n).transpose(0, 1, 3, 2))
    if fmt == "e4m3":
        words = by_word.astype(ml_dtypes.float8_e4m3fn).view(np.uint8)
    else:
        c = by_word.astype(ml_dtypes.float4_e2m1fn).view(np.uint8) & 0xF
        words = (c[..., 0::2] | (c[..., 1::2] << 4)).reshape(k // 512, 128, 2 * n)
    return np.ascontiguousarray(words), np.ascontiguousarray(byte.astype(np.uint8).reshape(k // 512, 16, n))


def unpack_weight(words, scales, fmt):
    g, _, n = scales.shape
    words = np.ascontiguousarray(words).reshape(g, 128, n, -1)
    if fmt == "e4m3":
        vals = words.view(ml_dtypes.float8_e4m3fn).astype(np.float64)
    else:
        nib = np.empty((g, 128, n, 4), np.uint8)
        nib[..., 0::2] = words & 0xF
        nib[..., 1::2] = words >> 4
        vals = E2M1[nib]
    vals = vals * np.repeat(np.exp2(scales.astype(np.float64) - 127.0), 8, axis=1)[..., None]
    return vals.transpose(0, 1, 3, 2).reshape(g * 512, n)


D, E, T, I, Q = 512, 512, 2048, 512, 128


def setup_inputs():
    n = np.random.standard_normal
    idx = np.random.permutation(T)[:I]
    fd = mx_kscale(D)
    fe = mx_kscale(E)
    keysp = pack_weight(n((D, T)) / fd[:, None], "e2m1")
    valsp = pack_weight(n((E, T)) / fe[:, None], "e2m1")
    return {
        "query": (n((D, Q)) * 1.0 / np.sqrt(D) * fd[:, None]).astype(np.float32),
        "keys_words": keysp[0],
        "keys_scales": keysp[1],
        "sharp": (np.random.uniform(0.4, 1.0, (Q, 1))).astype(np.float32),
        "gout": (n((E, Q)) * 1 / np.sqrt(E) * fe[:, None]).astype(np.float32),
        "vals_words": valsp[0],
        "vals_scales": valsp[1],
        "old": (0.5 * n((Q, T))).astype(np.float32),
        "offs": striped(idx),
    }


def reference(query, keys_words, keys_scales, sharp, gout, vals_words, vals_scales, old, offs):
    idx = unstriped(offs)
    keysu = unpack_weight(keys_words, keys_scales, "e2m1")
    valsu = unpack_weight(vals_words, vals_scales, "e2m1")
    queryq = mxq(f64(query), 0, "e4m3")
    keysidxg = keysu[:, idx]
    a = queryq.T @ keysidxg
    m1 = np.mean(a, axis=1, keepdims=True)
    ce = a - m1
    sd = np.sqrt(np.mean(np.square(ce), axis=1, keepdims=True) + 0.05)
    s = ce / sd * f64(sharp)
    p = np.exp(s - np.max(s, axis=1, keepdims=True))
    z = np.sum(p, axis=1, keepdims=True)
    goutq = mxq(f64(gout), 0, "e4m3")
    valsidxg = valsu[:, idx]
    c0 = goutq.T @ valsidxg
    dz = np.sum(c0 * p / np.square(z) * (-1.0), axis=1, keepdims=True)
    dp = c0 / z + dz
    ds = dp * p
    dsd = np.sum(ds * f64(sharp) * ce / np.square(sd) * (-1.0), axis=1, keepdims=True)
    dce = ds * f64(sharp) / sd + dsd * 0.5 / np.sqrt(np.mean(np.square(ce), axis=1, keepdims=True) + 0.05) / 512.0 * ce * 2.0
    dm1 = np.sum(dce * (-1.0), axis=1, keepdims=True)
    da = dce + dm1 / 512.0
    gs = da * 512.0
    gf = np.zeros((Q, T))
    gf[:, idx] = gs
    y = f64(old) + gf
    return y

@@ -1,0 +1,152 @@
+from contextlib import ExitStack
+
+import concourse.mybir as mybir
+
+D, E, T, I, Q = 512, 512, 2048, 512, 128
+FLOPS = 2 * Q * I * (D + E)
+
+F32 = mybir.dt.float32
+BF16 = mybir.dt.bfloat16
+I32 = mybir.dt.int32
+U32 = mybir.dt.uint32
+U16 = mybir.dt.uint16
+U8 = mybir.dt.uint8
+FP8X4 = mybir.dt.float8_e4m3fn_x4
+FP4X4 = mybir.dt.float4_e2m1fn_x4
+ALU = mybir.AluOpType
+ACT = mybir.ActivationFunctionType
+
+P = 128
+PACK = 4
+EPS = 0.05
+STORE_EDGES = (0, 256, 768, 1408, 2048)
+
+
+def tile_attend_bstandardised_s_kernel(tc, query, keys_words, keys_scales, sharp, gout, vals_words, vals_scales, old, offs, out):
+    nc = tc.nc
+    with ExitStack() as ctx:
+        sb = ctx.enter_context(tc.tile_pool(name="sb", bufs=1))
+        ps = ctx.enter_context(tc.psum_pool(name="ps", bufs=1))
+
+        def tile(name, shape, dtype):
+            return sb.tile(shape, dtype, name=name, align_bytes=64)
+
+        offsets = sb.tile([P, I // 16], U16, name="offsets")
+        kw = tile("kw", [P, T], U16)
+        ks = tile("ks", [P, T], U8)
+        vw = tile("vw", [P, T], U16)
+        vs = tile("vs", [P, T], U8)
+        q_raw = tile("q_raw", [P, PACK, Q], F32)
+        g_raw = tile("g_raw", [P, PACK, Q], F32)
+        sharp_in = tile("sharp_in", [P, 1], F32)
+        old_sb = tile("old_sb", [P, T], F32)
+        window = tile("window", [P, T], F32)
+        minus_half = tile("minus_half", [P, 1], F32)
+
+        nc.vector.memset(ks[:].bitcast(I32), 0)
+        nc.vector.memset(vs[:].bitcast(I32), 0)
+        nc.gpsimd.memset(minus_half[:], -0.5)
+        nc.vector.memset(window[:], 0.0)
+
+        def load_scales(eng, plane, rows):
+            for quad in range(4):
+                eng.dma_start(out=plane[32 * quad : 32 * quad + 4, :].bitcast(I32), in_=rows[0, 4 * quad : 4 * quad + 4, :].bitcast(I32))
+
+        nc.sync.dma_start(offsets[:], offs)
+        load_scales(nc.scalar, ks, keys_scales)
+        nc.sync.dma_start(out=kw[:].bitcast(I32), in_=keys_words[0].bitcast(I32))
+        nc.sync.dma_start(out=q_raw[:], in_=query.rearrange("(p j) w -> p j w", j=PACK))
+        nc.sync.dma_start(out=vw[:].bitcast(I32), in_=vals_words[0].bitcast(I32))
+        nc.sync.dma_start(out=sharp_in[:], in_=sharp)
+        load_scales(nc.sync, vs, vals_scales)
+        nc.sync.dma_start(out=g_raw[:], in_=gout.rearrange("(p j) w -> p j w", j=PACK))
+        nc.sync.dma_start(out=old_sb[:], in_=old)
+
+        def interleave(name, raw):
+            grouped = tile(name + "_bf", [P, Q, PACK], BF16)
+            nc.scalar.activation(grouped[:], raw[:].rearrange("p j w -> p w j"), ACT.Copy)
+            return grouped
+
+        def quantize(name, grouped):
+            codes = tile(name + "_codes", [P, Q], U32)
+            scales = tile(name + "_scales", [P, Q], U8)
+            nc.vector.quantize_mx(out=codes[:].bitcast(FP8X4), scales=scales[:], in_=grouped[:].rearrange("p w j -> p (w j)"))
+            return codes, scales
+
+        def gather(name, pool_tile, dtype):
+            got = tile(name, [P, I], dtype)
+            nc.vector.tensor_copy(got[:], pool_tile[:].indirect(offsets[:]))
+            return got
+
+        def product(name, codes, scales, words, word_scales):
+            acc = ps.tile([P, I], F32, name=name)
+            nc.tensor.matmul_mx(out=acc[:], lhsT=codes[:].bitcast(FP8X4), lhsT_scale=scales[:],
+                                rhs=words[:].bitcast(FP4X4), rhs_scale=word_scales[:], start=True, stop=True)
+            return acc
+
+        def col(name, n=1):
+            return tile(name, [P, n], F32)
+
+        ksg = gather("ksg", ks, U8)
+        kwg = gather("kwg", kw, U16)
+        q_codes, q_scales = quantize("q", interleave("q", q_raw))
+        a = product("a", q_codes, q_scales, kwg, ksg)
+
+        by_r = col("by_r", 3)
+        nsharp = col("nsharp")
+        nc.scalar.activation(by_r[:, 0:1], sharp_in[:], ACT.Copy)
+        nc.scalar.activation(by_r[:, 1:2], sharp_in[:], ACT.Copy, scale=float(I))
+        nc.scalar.activation(nsharp[:], sharp_in[:], ACT.Copy, scale=-float(I))
+
+        vwg = gather("vwg", vw, U16)
+        vsg = gather("vsg", vs, U8)
+        g_codes, g_scales = quantize("g", interleave("g", g_raw))
+        c0 = product("c0", g_codes, g_scales, vwg, vsg)
+
+        a_n = tile("a_n", [P, I], F32)
+        mean = col("mean")
+        nc.scalar.activation(a_n[:], a[:], ACT.Identity, scale=1.0 / I, accum_out=mean[:])
+        sq = tile("sq", [P, I], F32)
+        ss = col("ss")
+        nc.scalar.activation(sq[:], a[:], ACT.Square, scale=-1.0, bias=mean[:], accum_out=ss[:])
+        nce = tile("nce", [P, I], F32)
+        nc.scalar.activation(nce[:], a[:], ACT.Identity, scale=-1.0, bias=mean[:])
+        var = col("var")
+        r = col("r")
+        nc.gpsimd.tensor_scalar(var[:], ss[:], 1.0 / I, EPS, ALU.mult, ALU.add)
+        nc.gpsimd.tensor_tensor(r[:], var[:], minus_half[:], ALU.pow)
+        nt = tile("nt", [P, I], F32)
+        nc.vector.tensor_scalar(nt[:], a_n[:], nsharp[:], None, ALU.mult, ALU.min, accum_out=by_r[:, 2:3])
+        kb = col("kb", 4)
+        nc.scalar.activation(kb[:, 1:4], by_r[:], ACT.Copy, scale=r[:])
+        p = tile("p", [P, I], F32)
+        z = col("z")
+        nc.scalar.activation(p[:], a[:], ACT.Exp, scale=kb[:, 1:2], bias=kb[:, 3:4], accum_out=z[:])
+        nc.vector.tensor_scalar(kb[:, 0:1], kb[:, 1:2], r[:], r[:], ALU.mult, ALU.mult)
+
+        rz = col("rz")
+        nc.vector.reciprocal(rz[:], z[:])
+        ac = col("ac", 2)
+        nc.scalar.activation(ac[:], kb[:, 0:3:2], ACT.Copy, scale=rz[:])
+        pa = tile("pa", [P, I], F32)
+        nc.scalar.activation(pa[:], p[:], ACT.Copy, scale=ac[:, 1:2])
+
+        pce = tile("pce", [P, I], F32)
+        half = I // 2
+        nc.vector.scalar_tensor_tensor(pce[:, :half], a[:, :half], mean[:], p[:, :half], ALU.subtract, ALU.mult)
+        wc = tile("wc", [P, I], F32)
+        cbar = col("cbar")
+        nc.vector.scalar_tensor_tensor(wc[:], c0[:], rz[:], p[:], ALU.mult, ALU.mult, accum_out=cbar[:])
+        nc.vector.scalar_tensor_tensor(pce[:, half:], a[:, half:], mean[:], p[:, half:], ALU.subtract, ALU.mult)
+        uce = tile("uce", [P, I], F32)
+        su = col("su")
+        nc.vector.scalar_tensor_tensor(uce[:], c0[:], cbar[:], pce[:], ALU.subtract, ALU.mult, accum_out=su[:])
+        x = tile("x", [P, I], F32)
+        nc.vector.scalar_tensor_tensor(x[:], c0[:], cbar[:], pa[:], ALU.subtract, ALU.mult)
+        t = tile("t", [P, I], F32)
+        nc.vector.tensor_scalar(t[:], nce[:], su[:], ac[:, 0:1], ALU.mult, ALU.mult)
+        nc.vector.tensor_tensor(window[:].indirect(offsets[:]), x[:], t[:], ALU.add)
+
+        for lo, hi in zip(STORE_EDGES[:-1], STORE_EDGES[1:]):
+            nc.vector.tensor_tensor(old_sb[:, lo:hi], old_sb[:, lo:hi], window[:, lo:hi], ALU.add)
+            nc.sync.dma_start(out=out[:, lo:hi], in_=old_sb[:, lo:hi])

@@ -19,7 +19,7 @@ ACT = mybir.ActivationFunctionType
 P = 128
 PACK = 4
 EPS = 0.05
-STORE_EDGES = (0, 256, 768, 1408, 2048)
+STORE_EDGES = (0, 384, 896, 1472, 2048)
 
 
 def tile_attend_bstandardised_s_kernel(tc, query, keys_words, keys_scales, sharp, gout, vals_words, vals_scales, old, offs, out):
@@ -28,8 +28,8 @@ def tile_attend_bstandardised_s_kernel(tc, query, keys_words, keys_scales, sharp
         sb = ctx.enter_context(tc.tile_pool(name="sb", bufs=1))
         ps = ctx.enter_context(tc.psum_pool(name="ps", bufs=1))
 
-        def tile(name, shape, dtype):
-            return sb.tile(shape, dtype, name=name, align_bytes=64)
+        def tile(name, shape, dtype, tag=None):
+            return sb.tile(shape, dtype, name=name, tag=tag or name, align_bytes=64)
 
         offsets = sb.tile([P, I // 16], U16, name="offsets")
         kw = tile("kw", [P, T], U16)
@@ -43,28 +43,30 @@ def tile_attend_bstandardised_s_kernel(tc, query, keys_words, keys_scales, sharp
         window = tile("window", [P, T], F32)
         minus_half = tile("minus_half", [P, 1], F32)
 
-        nc.vector.memset(ks[:].bitcast(I32), 0)
-        nc.vector.memset(vs[:].bitcast(I32), 0)
-        nc.gpsimd.memset(minus_half[:], -0.5)
-        nc.vector.memset(window[:], 0.0)
+        nc.gpsimd.memset(ks[:].bitcast(I32), 0)
+        one = tile("one", [P, 1], F32)
+        nc.gpsimd.memset(one[:], 1.0)
+        nc.gpsimd.memset(vs[:].bitcast(I32), 0)
+        nc.gpsimd.dma_start(out=sharp_in[:], in_=sharp)
+        nc.gpsimd.memset(window[:], 0.0)
 
         def load_scales(eng, plane, rows):
             for quad in range(4):
                 eng.dma_start(out=plane[32 * quad : 32 * quad + 4, :].bitcast(I32), in_=rows[0, 4 * quad : 4 * quad + 4, :].bitcast(I32))
 
         nc.sync.dma_start(offsets[:], offs)
-        load_scales(nc.scalar, ks, keys_scales)
-        nc.sync.dma_start(out=kw[:].bitcast(I32), in_=keys_words[0].bitcast(I32))
+        load_scales(nc.sync, ks, keys_scales)
+        nc.scalar.activation(minus_half[:], one[:], ACT.Copy, scale=-0.5)
         nc.sync.dma_start(out=q_raw[:], in_=query.rearrange("(p j) w -> p j w", j=PACK))
+        nc.sync.dma_start(out=kw[:].bitcast(I32), in_=keys_words[0].bitcast(I32))
         nc.sync.dma_start(out=vw[:].bitcast(I32), in_=vals_words[0].bitcast(I32))
-        nc.sync.dma_start(out=sharp_in[:], in_=sharp)
         load_scales(nc.sync, vs, vals_scales)
         nc.sync.dma_start(out=g_raw[:], in_=gout.rearrange("(p j) w -> p j w", j=PACK))
         nc.sync.dma_start(out=old_sb[:], in_=old)
 
-        def interleave(name, raw):
-            grouped = tile(name + "_bf", [P, Q, PACK], BF16)
-            nc.scalar.activation(grouped[:], raw[:].rearrange("p j w -> p w j"), ACT.Copy)
+        def interleave(name, raw, tag=None):
+            grouped = tile(name + "_bf", [P, Q, PACK], BF16, tag)
+            nc.scalar.copy(grouped[:], raw[:].rearrange("p j w -> p w j"))
             return grouped
 
         def quantize(name, grouped):
@@ -84,24 +86,26 @@ def tile_attend_bstandardised_s_kernel(tc, query, keys_words, keys_scales, sharp
                                 rhs=words[:].bitcast(FP4X4), rhs_scale=word_scales[:], start=True, stop=True)
             return acc
 
-        def col(name, n=1):
-            return tile(name, [P, n], F32)
+        def col(name, n=1, tag=None):
+            return tile(name, [P, n], F32, tag)
 
+        half = I // 2
         ksg = gather("ksg", ks, U8)
-        kwg = gather("kwg", kw, U16)
         q_codes, q_scales = quantize("q", interleave("q", q_raw))
-        a = product("a", q_codes, q_scales, kwg, ksg)
+        kwg = tile("kwg", [P, I], U16)
+        a = ps.tile([P, I], F32, name="a")
+        for h in range(2):
+            cols = slice(h * half, (h + 1) * half)
+            nc.vector.tensor_copy(kwg[:, cols], kw[:].indirect(offsets[:, h * half // 16 : (h + 1) * half // 16]))
+            nc.tensor.matmul_mx(out=a[:, cols], lhsT=q_codes[:].bitcast(FP8X4), lhsT_scale=q_scales[:],
+                                rhs=kwg[:, cols].bitcast(FP4X4), rhs_scale=ksg[:, cols], start=True, stop=True)
 
-        by_r = col("by_r", 3)
-        nsharp = col("nsharp")
-        nc.scalar.activation(by_r[:, 0:1], sharp_in[:], ACT.Copy)
-        nc.scalar.activation(by_r[:, 1:2], sharp_in[:], ACT.Copy, scale=float(I))
-        nc.scalar.activation(nsharp[:], sharp_in[:], ACT.Copy, scale=-float(I))
+        by_r = col("by_r", 4, "q_raw")
+        nc.scalar.activation(by_r[:, 0:1], sharp_in[:], ACT.Copy, scale=float(I))
+        nc.scalar.activation(by_r[:, 2:3], sharp_in[:], ACT.Copy, scale=-float(I))
 
         vwg = gather("vwg", vw, U16)
         vsg = gather("vsg", vs, U8)
-        g_codes, g_scales = quantize("g", interleave("g", g_raw))
-        c0 = product("c0", g_codes, g_scales, vwg, vsg)
 
         a_n = tile("a_n", [P, I], F32)
         mean = col("mean")
@@ -109,30 +113,35 @@ def tile_attend_bstandardised_s_kernel(tc, query, keys_words, keys_scales, sharp
         sq = tile("sq", [P, I], F32)
         ss = col("ss")
         nc.scalar.activation(sq[:], a[:], ACT.Square, scale=-1.0, bias=mean[:], accum_out=ss[:])
-        nce = tile("nce", [P, I], F32)
-        nc.scalar.activation(nce[:], a[:], ACT.Identity, scale=-1.0, bias=mean[:])
         var = col("var")
         r = col("r")
-        nc.gpsimd.tensor_scalar(var[:], ss[:], 1.0 / I, EPS, ALU.mult, ALU.add)
+        nc.scalar.activation(var[:], ss[:], ACT.Copy, scale=1.0 / I, bias=EPS)
         nc.gpsimd.tensor_tensor(r[:], var[:], minus_half[:], ALU.pow)
+        nc.scalar.activation(by_r[:, 3:4], sharp_in[:], ACT.Copy, scale=mean[:])
+        g_bf = interleave("g", g_raw, "ss")
         nt = tile("nt", [P, I], F32)
-        nc.vector.tensor_scalar(nt[:], a_n[:], nsharp[:], None, ALU.mult, ALU.min, accum_out=by_r[:, 2:3])
+        nc.vector.tensor_scalar(nt[:], a_n[:], by_r[:, 2:3], None, ALU.mult, ALU.min, accum_out=by_r[:, 1:2])
+        g_codes, g_scales = quantize("g", g_bf)
+        c0 = product("c0", g_codes, g_scales, vwg, vsg)
         kb = col("kb", 4)
-        nc.scalar.activation(kb[:, 1:4], by_r[:], ACT.Copy, scale=r[:])
+        nc.scalar.activation(kb[:], by_r[:], ACT.Copy, scale=r[:])
         p = tile("p", [P, I], F32)
         z = col("z")
-        nc.scalar.activation(p[:], a[:], ACT.Exp, scale=kb[:, 1:2], bias=kb[:, 3:4], accum_out=z[:])
-        nc.vector.tensor_scalar(kb[:, 0:1], kb[:, 1:2], r[:], r[:], ALU.mult, ALU.mult)
+        nc.scalar.activation(p[:], a_n[:], ACT.Exp, scale=kb[:, 0:1], bias=kb[:, 1:2], accum_out=z[:])
+        kr2 = col("kr2", 2)
+        nc.vector.tensor_scalar(kr2[:], kb[:, 2:4], r[:], r[:], ALU.mult, ALU.mult)
 
         rz = col("rz")
         nc.vector.reciprocal(rz[:], z[:])
-        ac = col("ac", 2)
-        nc.scalar.activation(ac[:], kb[:, 0:3:2], ACT.Copy, scale=rz[:])
+        ac = col("ac", 3)
+        nc.scalar.activation(ac[:, 0:1], kb[:, 0:1], ACT.Copy, scale=rz[:])
+        nc.scalar.activation(ac[:, 1:3], kr2[:], ACT.Copy, scale=rz[:])
         pa = tile("pa", [P, I], F32)
-        nc.scalar.activation(pa[:], p[:], ACT.Copy, scale=ac[:, 1:2])
+        nc.scalar.activation(pa[:], p[:], ACT.Copy, scale=ac[:, 0:1])
+        ncek = tile("ncek", [P, I], F32)
+        nc.scalar.activation(ncek[:], a_n[:], ACT.Identity, scale=ac[:, 1:2], bias=ac[:, 2:3])
 
         pce = tile("pce", [P, I], F32)
-        half = I // 2
         nc.vector.scalar_tensor_tensor(pce[:, :half], a[:, :half], mean[:], p[:, :half], ALU.subtract, ALU.mult)
         wc = tile("wc", [P, I], F32)
         cbar = col("cbar")
@@ -144,7 +153,7 @@ def tile_attend_bstandardised_s_kernel(tc, query, keys_words, keys_scales, sharp
         x = tile("x", [P, I], F32)
         nc.vector.scalar_tensor_tensor(x[:], c0[:], cbar[:], pa[:], ALU.subtract, ALU.mult)
         t = tile("t", [P, I], F32)
-        nc.vector.tensor_scalar(t[:], nce[:], su[:], ac[:, 0:1], ALU.mult, ALU.mult)
+        nc.scalar.activation(t[:], ncek[:], ACT.Copy, scale=su[:])
         nc.vector.tensor_tensor(window[:].indirect(offsets[:]), x[:], t[:], ALU.add)
 
         for lo, hi in zip(STORE_EDGES[:-1], STORE_EDGES[1:]):

@@ -46,22 +46,22 @@ def tile_attend_bstandardised_s_kernel(tc, query, keys_words, keys_scales, sharp
         nc.gpsimd.memset(ks[:].bitcast(I32), 0)
         one = tile("one", [P, 1], F32)
         nc.gpsimd.memset(one[:], 1.0)
-        nc.gpsimd.memset(vs[:].bitcast(I32), 0)
+        nc.vector.memset(vs[:].bitcast(I32), 0)
         nc.gpsimd.dma_start(out=sharp_in[:], in_=sharp)
         nc.gpsimd.memset(window[:], 0.0)
 
         def load_scales(eng, plane, rows):
-            for quad in range(4):
-                eng.dma_start(out=plane[32 * quad : 32 * quad + 4, :].bitcast(I32), in_=rows[0, 4 * quad : 4 * quad + 4, :].bitcast(I32))
+            for j in range(4):
+                eng.dma_start(out=plane[j:P:32, :].bitcast(I32), in_=rows[0, j:16:4, :].bitcast(I32))
 
         nc.sync.dma_start(offsets[:], offs)
         load_scales(nc.sync, ks, keys_scales)
         nc.scalar.activation(minus_half[:], one[:], ACT.Copy, scale=-0.5)
         nc.sync.dma_start(out=q_raw[:], in_=query.rearrange("(p j) w -> p j w", j=PACK))
         nc.sync.dma_start(out=kw[:].bitcast(I32), in_=keys_words[0].bitcast(I32))
+        nc.sync.dma_start(out=g_raw[:], in_=gout.rearrange("(p j) w -> p j w", j=PACK))
         nc.sync.dma_start(out=vw[:].bitcast(I32), in_=vals_words[0].bitcast(I32))
         load_scales(nc.sync, vs, vals_scales)
-        nc.sync.dma_start(out=g_raw[:], in_=gout.rearrange("(p j) w -> p j w", j=PACK))
         nc.sync.dma_start(out=old_sb[:], in_=old)
 
         def interleave(name, raw, tag=None):
@@ -104,8 +104,10 @@ def tile_attend_bstandardised_s_kernel(tc, query, keys_words, keys_scales, sharp
         nc.scalar.activation(by_r[:, 0:1], sharp_in[:], ACT.Copy, scale=float(I))
         nc.scalar.activation(by_r[:, 2:3], sharp_in[:], ACT.Copy, scale=-float(I))
 
+        g_codes, g_scales = quantize("g", interleave("g", g_raw))
         vwg = gather("vwg", vw, U16)
-        vsg = gather("vsg", vs, U8)
+        vsg0 = tile("vsg0", [P, half], U8)
+        nc.vector.tensor_copy(vsg0[:], vs[:].indirect(offsets[:, : half // 16]))
 
         a_n = tile("a_n", [P, I], F32)
         mean = col("mean")
@@ -118,11 +120,15 @@ def tile_attend_bstandardised_s_kernel(tc, query, keys_words, keys_scales, sharp
         nc.scalar.activation(var[:], ss[:], ACT.Copy, scale=1.0 / I, bias=EPS)
         nc.gpsimd.tensor_tensor(r[:], var[:], minus_half[:], ALU.pow)
         nc.scalar.activation(by_r[:, 3:4], sharp_in[:], ACT.Copy, scale=mean[:])
-        g_bf = interleave("g", g_raw, "ss")
         nt = tile("nt", [P, I], F32)
         nc.vector.tensor_scalar(nt[:], a_n[:], by_r[:, 2:3], None, ALU.mult, ALU.min, accum_out=by_r[:, 1:2])
-        g_codes, g_scales = quantize("g", g_bf)
-        c0 = product("c0", g_codes, g_scales, vwg, vsg)
+        vsg1 = tile("vsg1", [P, half], U8, "sq")
+        nc.vector.tensor_copy(vsg1[:], vs[:].indirect(offsets[:, half // 16 :]))
+        c0 = ps.tile([P, I], F32, name="c0")
+        for h, vsg in enumerate((vsg0, vsg1)):
+            cols = slice(h * half, (h + 1) * half)
+            nc.tensor.matmul_mx(out=c0[:, cols], lhsT=g_codes[:].bitcast(FP8X4), lhsT_scale=g_scales[:],
+                                rhs=vwg[:, cols].bitcast(FP4X4), rhs_scale=vsg[:], start=True, stop=True)
         kb = col("kb", 4)
         nc.scalar.activation(kb[:], by_r[:], ACT.Copy, scale=r[:])
         p = tile("p", [P, I], F32)

from contextlib import ExitStack

import concourse.mybir as mybir

D, E, T, I, Q = 512, 512, 2048, 512, 128
FLOPS = 2 * Q * I * (D + E)

F32 = mybir.dt.float32
BF16 = mybir.dt.bfloat16
I32 = mybir.dt.int32
U32 = mybir.dt.uint32
U16 = mybir.dt.uint16
U8 = mybir.dt.uint8
FP8X4 = mybir.dt.float8_e4m3fn_x4
FP4X4 = mybir.dt.float4_e2m1fn_x4
ALU = mybir.AluOpType
ACT = mybir.ActivationFunctionType

P = 128
PACK = 4
EPS = 0.05
STORE_EDGES = (0, 384, 896, 1472, 2048)


def tile_attend_bstandardised_s_kernel(tc, query, keys_words, keys_scales, sharp, gout, vals_words, vals_scales, old, offs, out):
    nc = tc.nc
    with ExitStack() as ctx:
        sb = ctx.enter_context(tc.tile_pool(name="sb", bufs=1))
        ps = ctx.enter_context(tc.psum_pool(name="ps", bufs=1))

        def tile(name, shape, dtype, tag=None):
            return sb.tile(shape, dtype, name=name, tag=tag or name, align_bytes=64)

        offsets = sb.tile([P, I // 16], U16, name="offsets")
        kw = tile("kw", [P, T], U16)
        ks = tile("ks", [P, T], U8)
        vw = tile("vw", [P, T], U16)
        vs = tile("vs", [P, T], U8)
        q_raw = tile("q_raw", [P, PACK, Q], F32)
        g_raw = tile("g_raw", [P, PACK, Q], F32)
        sharp_in = tile("sharp_in", [P, 1], F32)
        old_sb = tile("old_sb", [P, T], F32)
        window = tile("window", [P, T], F32)
        minus_half = tile("minus_half", [P, 1], F32)

        nc.gpsimd.memset(ks[:].bitcast(I32), 0)
        one = tile("one", [P, 1], F32)
        nc.gpsimd.memset(one[:], 1.0)
        nc.vector.memset(vs[:].bitcast(I32), 0)
        nc.gpsimd.dma_start(out=sharp_in[:], in_=sharp)
        nc.gpsimd.memset(window[:], 0.0)

        def load_scales(eng, plane, rows):
            for j in range(4):
                eng.dma_start(out=plane[j:P:32, :].bitcast(I32), in_=rows[0, j:16:4, :].bitcast(I32))

        nc.sync.dma_start(offsets[:], offs)
        load_scales(nc.sync, ks, keys_scales)
        nc.scalar.activation(minus_half[:], one[:], ACT.Copy, scale=-0.5)
        nc.sync.dma_start(out=q_raw[:], in_=query.rearrange("(p j) w -> p j w", j=PACK))
        nc.sync.dma_start(out=kw[:].bitcast(I32), in_=keys_words[0].bitcast(I32))
        nc.sync.dma_start(out=g_raw[:], in_=gout.rearrange("(p j) w -> p j w", j=PACK))
        nc.sync.dma_start(out=vw[:].bitcast(I32), in_=vals_words[0].bitcast(I32))
        load_scales(nc.sync, vs, vals_scales)
        nc.sync.dma_start(out=old_sb[:], in_=old)

        def interleave(name, raw, tag=None):
            grouped = tile(name + "_bf", [P, Q, PACK], BF16, tag)
            nc.scalar.copy(grouped[:], raw[:].rearrange("p j w -> p w j"))
            return grouped

        def quantize(name, grouped):
            codes = tile(name + "_codes", [P, Q], U32)
            scales = tile(name + "_scales", [P, Q], U8)
            nc.vector.quantize_mx(out=codes[:].bitcast(FP8X4), scales=scales[:], in_=grouped[:].rearrange("p w j -> p (w j)"))
            return codes, scales

        def gather(name, pool_tile, dtype):
            got = tile(name, [P, I], dtype)
            nc.vector.tensor_copy(got[:], pool_tile[:].indirect(offsets[:]))
            return got

        def product(name, codes, scales, words, word_scales):
            acc = ps.tile([P, I], F32, name=name)
            nc.tensor.matmul_mx(out=acc[:], lhsT=codes[:].bitcast(FP8X4), lhsT_scale=scales[:],
                                rhs=words[:].bitcast(FP4X4), rhs_scale=word_scales[:], start=True, stop=True)
            return acc

        def col(name, n=1, tag=None):
            return tile(name, [P, n], F32, tag)

        half = I // 2
        ksg = gather("ksg", ks, U8)
        q_codes, q_scales = quantize("q", interleave("q", q_raw))
        kwg = tile("kwg", [P, I], U16)
        a = ps.tile([P, I], F32, name="a")
        for h in range(2):
            cols = slice(h * half, (h + 1) * half)
            nc.vector.tensor_copy(kwg[:, cols], kw[:].indirect(offsets[:, h * half // 16 : (h + 1) * half // 16]))
            nc.tensor.matmul_mx(out=a[:, cols], lhsT=q_codes[:].bitcast(FP8X4), lhsT_scale=q_scales[:],
                                rhs=kwg[:, cols].bitcast(FP4X4), rhs_scale=ksg[:, cols], start=True, stop=True)

        by_r = col("by_r", 4, "q_raw")
        nc.scalar.activation(by_r[:, 0:1], sharp_in[:], ACT.Copy, scale=float(I))
        nc.scalar.activation(by_r[:, 2:3], sharp_in[:], ACT.Copy, scale=-float(I))

        g_codes, g_scales = quantize("g", interleave("g", g_raw))
        vwg = gather("vwg", vw, U16)
        vsg0 = tile("vsg0", [P, half], U8)
        nc.vector.tensor_copy(vsg0[:], vs[:].indirect(offsets[:, : half // 16]))

        a_n = tile("a_n", [P, I], F32)
        mean = col("mean")
        nc.scalar.activation(a_n[:], a[:], ACT.Identity, scale=1.0 / I, accum_out=mean[:])
        sq = tile("sq", [P, I], F32)
        ss = col("ss")
        nc.scalar.activation(sq[:], a[:], ACT.Square, scale=-1.0, bias=mean[:], accum_out=ss[:])
        var = col("var")
        r = col("r")
        nc.scalar.activation(var[:], ss[:], ACT.Copy, scale=1.0 / I, bias=EPS)
        nc.gpsimd.tensor_tensor(r[:], var[:], minus_half[:], ALU.pow)
        nc.scalar.activation(by_r[:, 3:4], sharp_in[:], ACT.Copy, scale=mean[:])
        nt = tile("nt", [P, I], F32)
        nc.vector.tensor_scalar(nt[:], a_n[:], by_r[:, 2:3], None, ALU.mult, ALU.min, accum_out=by_r[:, 1:2])
        vsg1 = tile("vsg1", [P, half], U8, "sq")
        nc.vector.tensor_copy(vsg1[:], vs[:].indirect(offsets[:, half // 16 :]))
        c0 = ps.tile([P, I], F32, name="c0")
        for h, vsg in enumerate((vsg0, vsg1)):
            cols = slice(h * half, (h + 1) * half)
            nc.tensor.matmul_mx(out=c0[:, cols], lhsT=g_codes[:].bitcast(FP8X4), lhsT_scale=g_scales[:],
                                rhs=vwg[:, cols].bitcast(FP4X4), rhs_scale=vsg[:], start=True, stop=True)
        kb = col("kb", 4)
        nc.scalar.activation(kb[:], by_r[:], ACT.Copy, scale=r[:])
        p = tile("p", [P, I], F32)
        z = col("z")
        nc.scalar.activation(p[:], a_n[:], ACT.Exp, scale=kb[:, 0:1], bias=kb[:, 1:2], accum_out=z[:])
        kr2 = col("kr2", 2)
        nc.vector.tensor_scalar(kr2[:], kb[:, 2:4], r[:], r[:], ALU.mult, ALU.mult)

        rz = col("rz")
        nc.vector.reciprocal(rz[:], z[:])
        ac = col("ac", 3)
        nc.scalar.activation(ac[:, 0:1], kb[:, 0:1], ACT.Copy, scale=rz[:])
        nc.scalar.activation(ac[:, 1:3], kr2[:], ACT.Copy, scale=rz[:])
        pa = tile("pa", [P, I], F32)
        nc.scalar.activation(pa[:], p[:], ACT.Copy, scale=ac[:, 0:1])
        ncek = tile("ncek", [P, I], F32)
        nc.scalar.activation(ncek[:], a_n[:], ACT.Identity, scale=ac[:, 1:2], bias=ac[:, 2:3])

        pce = tile("pce", [P, I], F32)
        nc.vector.scalar_tensor_tensor(pce[:, :half], a[:, :half], mean[:], p[:, :half], ALU.subtract, ALU.mult)
        wc = tile("wc", [P, I], F32)
        cbar = col("cbar")
        nc.vector.scalar_tensor_tensor(wc[:], c0[:], rz[:], p[:], ALU.mult, ALU.mult, accum_out=cbar[:])
        nc.vector.scalar_tensor_tensor(pce[:, half:], a[:, half:], mean[:], p[:, half:], ALU.subtract, ALU.mult)
        uce = tile("uce", [P, I], F32)
        su = col("su")
        nc.vector.scalar_tensor_tensor(uce[:], c0[:], cbar[:], pce[:], ALU.subtract, ALU.mult, accum_out=su[:])
        x = tile("x", [P, I], F32)
        nc.vector.scalar_tensor_tensor(x[:], c0[:], cbar[:], pa[:], ALU.subtract, ALU.mult)
        t = tile("t", [P, I], F32)
        nc.scalar.activation(t[:], ncek[:], ACT.Copy, scale=su[:])
        nc.vector.tensor_tensor(window[:].indirect(offsets[:]), x[:], t[:], ALU.add)

        for lo, hi in zip(STORE_EDGES[:-1], STORE_EDGES[1:]):
            nc.vector.tensor_tensor(old_sb[:, lo:hi], old_sb[:, lo:hi], window[:, lo:hi], ALU.add)
            nc.sync.dma_start(out=out[:, lo:hi], in_=old_sb[:, lo:hi])
